import numpy as np
import ml_dtypes


def mxq(x, axis, fmt="e4m3"):
    dtype, down = {"e4m3": (ml_dtypes.float8_e4m3fn, 7), "e5m2": (ml_dtypes.float8_e5m2, 14)}[fmt]
    v = np.moveaxis(np.asarray(x, np.float32).astype(ml_dtypes.bfloat16).astype(np.float64), axis, -1)
    blocks = v.reshape(v.shape[:-1] + (-1, 32))
    amax = np.abs(blocks).max(-1, keepdims=True)
    byte = np.maximum(np.where(amax > 0, np.frexp(amax)[1] - 1 + 127, 0) - down, 1)
    scale = np.exp2(byte - 127.0)
    codes = (blocks / scale).astype(np.float32).astype(dtype).astype(np.float64)
    return np.moveaxis((codes * scale).reshape(v.shape), -1, axis)


WIDE = False


def mx_kscale(k):
    if not WIDE:
        return np.ones(k)
    levels = np.array([10, -10, 5, -5, 0])
    if k % 512:
        return np.exp2(np.random.permutation(np.resize(levels, k // 32))).repeat(32)
    a = np.empty((k // 512, 16))
    for p in range(k // 512):
        a[p, :8] = np.random.permutation(np.resize(levels, 8))
        for g in range(8):
            far = levels[np.abs(levels - a[p, g]) >= 10]
            a[p, g + 8] = far[np.random.randint(len(far))]
    return np.exp2(a.ravel()).repeat(32)


def f64(x):
    return np.asarray(x).astype(np.float64)


def striped8(idx):
    return np.concatenate([v.reshape(-1, 16).T for v in idx]).astype(np.uint16)


def unstriped8(offs):
    return np.stack([offs[16 * g:16 * g + 16].T.reshape(-1) for g in range(8)]).astype(np.int64)


E2M1 = np.array([0.0, 0.5, 1.0, 1.5, 2.0, 3.0, 4.0, 6.0, -0.0, -0.5, -1.0, -1.5, -2.0, -3.0, -4.0, -6.0])


def pack_weight(w, fmt):
    k, n = w.shape
    w = f64(np.asarray(w, np.float32).astype(ml_dtypes.bfloat16)).reshape(k // 32, 32, n)
    amax = np.abs(w).max(1)
    if fmt == "e4m3":
        byte = np.frexp(amax)[1] - 1 + 127 - 7
    else:
        mant, ex = np.frexp(amax / 6.0)
        byte = np.where(mant > 0.5, ex, ex - 1) + 127
    byte = np.clip(np.where(amax > 0, byte, 1), 1, 254)
    scaled = (w * np.exp2(127.0 - byte)[:, None, :]).reshape(k, n).astype(np.float32)
    by_word = np.ascontiguousarray(scaled.reshape(k // 512, 128, 4, n).transpose(0, 1, 3, 2))
    if fmt == "e4m3":
        words = by_word.astype(ml_dtypes.float8_e4m3fn).view(np.uint8)
    else:
        c = by_word.astype(ml_dtypes.float4_e2m1fn).view(np.uint8) & 0xF
        words = (c[..., 0::2] | (c[..., 1::2] << 4)).reshape(k // 512, 128, 2 * n)
    return np.ascontiguousarray(words), np.ascontiguousarray(byte.astype(np.uint8).reshape(k // 512, 16, n))


def unpack_weight(words, scales, fmt):
    g, _, n = scales.shape
    words = np.ascontiguousarray(words).reshape(g, 128, n, -1)
    if fmt == "e4m3":
        vals = words.view(ml_dtypes.float8_e4m3fn).astype(np.float64)
    else:
        nib = np.empty((g, 128, n, 4), np.uint8)
        nib[..., 0::2] = words & 0xF
        nib[..., 1::2] = words >> 4
        vals = E2M1[nib]
    vals = vals * np.repeat(np.exp2(scales.astype(np.float64) - 127.0), 8, axis=1)[..., None]
    return vals.transpose(0, 1, 3, 2).reshape(g * 512, n)


def gelu(v):
    return 0.5 * v * (1.0 + np.tanh(np.sqrt(2.0 / np.pi) * (v + 0.044715 * v**3)))


K, L, M, T, S = 512, 1024, 512, 2048, 512


def setup_inputs():
    n = np.random.standard_normal
    s1 = mx_kscale(K)[:, None]
    s2 = mx_kscale(L)[:, None]
    p_w4 = pack_weight(n((K, M)) / np.sqrt(K) / s1, "e2m1")
    return {
        "xT": (n((K, T)) * s1).astype(np.float32),
        "w4_words": p_w4[0],
        "w4_scales": p_w4[1],
        "c": (n((L, S)) * s2).astype(np.float32),
        "u": (n((L, M)) / np.sqrt(L) / s2).astype(np.float32),
        "wgt": np.repeat(np.random.uniform(0.5, 2.0, (8, S)), 16, axis=0).astype(np.float32),
        "b": (0.3 * n(512)).astype(np.float32),
        "offs": striped8(np.stack([np.random.permutation(T)[:S] for _ in range(8)])),
    }


def reference(xT, w4_words, w4_scales, c, u, wgt, b, offs):
    idx = unstriped8(offs)
    group = np.arange(K) % 512 // 64
    xg = f64(wgt)[np.arange(K) // 4 % 128] * f64(xT)[np.arange(K)[:, None], idx[group]]
    xT_ = mxq(xg, 0, "e4m3")
    w4_ = unpack_weight(w4_words, w4_scales, "e2m1")
    c_ = mxq(f64(c), 0, "e4m3")
    u_ = mxq(f64(u), 0, "e4m3")
    y = xT_.T @ w4_ + c_.T @ u_
    return gelu(y + f64(b)[None, :])

@@ -1,0 +1,215 @@
+from contextlib import ExitStack
+
+import concourse.mybir as mybir
+from concourse.masks import make_identity
+
+K, L, M, T, S = 512, 1024, 512, 2048, 512
+FLOPS = 2 * S * M * (K + L)
+
+F32 = mybir.dt.float32
+BF16 = mybir.dt.bfloat16
+I32 = mybir.dt.int32
+U32 = mybir.dt.uint32
+U16 = mybir.dt.uint16
+U8 = mybir.dt.uint8
+FP8X4 = mybir.dt.float8_e4m3fn_x4
+FP4X4 = mybir.dt.float4_e2m1fn_x4
+ADD = mybir.AluOpType.add
+MULT = mybir.AluOpType.mult
+COPY = mybir.ActivationFunctionType.Copy
+GELU = mybir.ActivationFunctionType.Gelu_apprx_tanh
+
+P = 128
+PACK = 4
+KP = P * PACK
+HALF = 256
+J = 128
+
+
+def tile_list_hmix_tm_gelu_kernel(tc, xT, w4_words, w4_scales, c, u, wgt, b, offs, out):
+    nc = tc.nc
+    with ExitStack() as ctx:
+        lists = ctx.enter_context(tc.tile_pool(name="lists", bufs=1))
+        keep = ctx.enter_context(tc.tile_pool(name="keep", bufs=1))
+        psum = ctx.enter_context(tc.psum_pool(name="psum", bufs=1))
+
+        def interleave(engine, dst, src):
+            o = dst.rearrange("p (a e) i -> p a i e", e=4)
+            s = src.rearrange("p i (a e) -> p a i e", e=4)
+            if engine == "v":
+                nc.vector.tensor_copy(out=o, in_=s)
+            else:
+                nc.scalar.activation(o, s, COPY)
+
+        def quantize(codes, scales, grouped):
+            nc.vector.quantize_mx(
+                out=codes.bitcast(FP8X4), scales=scales, in_=grouped.rearrange("p w i -> p (w i)")
+            )
+
+        offsets = lists.tile([P, S // 16], U16, name="offsets")
+        nc.sync.dma_start(offsets[:], offs)
+        wgt_sb = keep.tile([P, S], F32, name="wgt_sb")
+        nc.sync.dma_start(out=wgt_sb[:], in_=wgt)
+
+        x_rows = xT.rearrange("(p i) t -> p i t", i=PACK)
+        planes = [keep.tile([P, T], F32, name=f"plane{i}") for i in range(PACK)]
+
+        def load_plane(i):
+            nc.sync.dma_start(out=planes[i][:], in_=x_rows[:, i, :])
+
+        def load_rows(name, src, a, cols):
+            t = keep.tile([P, PACK, cols.stop - cols.start], F32, name=name)
+            rows = src[a * KP : (a + 1) * KP, cols].rearrange("(p i) w -> p i w", i=PACK)
+            nc.sync.dma_start(out=t[:], in_=rows)
+            return t
+
+        w4_sc = keep.tile([P, M], U8, name="w4_sc", align_bytes=64)
+        nc.gpsimd.memset(w4_sc[:].bitcast(I32), 0)
+        b_rows = keep.tile([P, P], F32, name="b_rows")
+        nc.gpsimd.memset(b_rows[:], 0.0)
+        ident = keep.tile([P, P], F32, name="ident")
+        make_identity(nc, ident[:])
+
+        load_plane(0)
+        u0_raw = load_rows("u0_raw", u, 0, slice(0, M))
+        load_plane(1)
+        load_plane(2)
+        w4_sb = keep.tile([P, 2 * M], U8, name="w4_sb", align_bytes=64)
+        nc.sync.dma_start(out=w4_sb[:].bitcast(I32), in_=w4_words[0].bitcast(I32))
+        for q in range(4):
+            nc.sync.dma_start(
+                out=w4_sc[32 * q : 32 * q + 4, :].bitcast(I32),
+                in_=w4_scales[0, 4 * q : 4 * q + 4, :].bitcast(I32),
+            )
+        nc.sync.dma_start(out=b_rows[0:4, :], in_=b.rearrange("(m n) -> m n", n=P))
+        load_plane(3)
+        c0_raw = load_rows("c0_raw", c, 0, slice(0, S))
+        u1_raw = load_rows("u1_raw", u, 1, slice(0, M))
+        c1_cols = [slice(0, 256), slice(256, 384), slice(384, 512)]
+        c1_raw = [load_rows(f"c1_raw{n}", c, 1, cols) for n, cols in enumerate(c1_cols)]
+
+        warm = keep.tile([P, 1], F32, name="warm")
+        nc.vector.memset(warm[:], 0.0)
+        warm_out = keep.tile([P, 1], F32, name="warm_out")
+        nc.scalar.activation(warm_out[:], warm[:], GELU)
+
+        def codes_and_scales(name):
+            return (
+                keep.tile([P, 512], U32, name=name + "_codes", align_bytes=64),
+                keep.tile([P, 512], U8, name=name + "_scales", align_bytes=64),
+            )
+
+        xg_q = codes_and_scales("xg")
+        u_q = [codes_and_scales(f"u{a}") for a in range(2)]
+        c_q = [codes_and_scales(f"c{a}") for a in range(2)]
+
+        def grouped_tile(name, w):
+            return keep.tile([P, w, PACK], BF16, name=name, align_bytes=64)
+
+        def quantize_into(q, cols, grouped):
+            quantize(q[0][:, cols], q[1][:, cols], grouped[:])
+
+        picked = [keep.tile([P, PACK, HALF], F32, name=f"picked{h}") for h in range(2)]
+
+        def gather(i, h):
+            nc.vector.tensor_tensor(
+                picked[h][:, i, :],
+                planes[i][:].indirect(offsets[:, 16 * h : 16 * (h + 1)]),
+                wgt_sb[:, HALF * h : HALF * (h + 1)],
+                MULT,
+            )
+
+        lo, hi = slice(0, HALF), slice(HALF, 512)
+
+        gather(0, 0)
+        gather(0, 1)
+        u0_g = grouped_tile("u0_g", 512)
+        interleave("s", u0_g[:], u0_raw[:])
+        gather(1, 0)
+        gather(1, 1)
+        quantize_into(u_q[0], slice(0, 512), u0_g)
+        gather(2, 0)
+        gather(2, 1)
+
+        b_bank = psum.tile([P, 512], F32, name="b_bank")
+        nc.tensor.transpose(b_bank[:, 0:P], b_rows[:], ident[:])
+        b_col = keep.tile([P, 4], F32, name="b_col")
+        nc.scalar.copy(b_col[:], b_bank[:, 0:4])
+        b_bank2 = psum.tile([P, 512], F32, name="b_bank2")
+        for m in range(4):
+            nc.tensor.transpose(
+                b_bank2[:, P * m : P * (m + 1)], b_col[:, m : m + 1].to_broadcast([P, P]), ident[:]
+            )
+        bias = keep.tile([P, M], F32, name="bias")
+        nc.scalar.copy(bias[:], b_bank2[:])
+
+        gather(3, 0)
+        xg_g = [grouped_tile(f"xg_g{h}", HALF) for h in range(2)]
+        interleave("s", xg_g[0][:], picked[0][:])
+        gather(3, 1)
+        interleave("v", xg_g[1][:], picked[1][:])
+        quantize_into(xg_q, lo, xg_g[0])
+        quantize_into(xg_q, hi, xg_g[1])
+
+        acc = [psum.tile([P, M], F32, name=f"acc{j}") for j in range(4)]
+
+        def mm(j, stat, mov, mov_scale, start, stop):
+            js = slice(J * j, J * (j + 1))
+            nc.tensor.matmul_mx(
+                out=acc[j][:],
+                lhsT=stat[0][:, js].bitcast(FP8X4),
+                lhsT_scale=stat[1][:, js],
+                rhs=mov,
+                rhs_scale=mov_scale,
+                start=start,
+                stop=stop,
+            )
+
+        for j in range(4):
+            mm(j, xg_q, w4_sb[:].bitcast(FP4X4), w4_sc[:], True, False)
+
+        c0_g = [grouped_tile(f"c0_g{h}", HALF) for h in range(2)]
+        interleave("s", c0_g[0][:], c0_raw[:, :, lo])
+        interleave("v", c0_g[1][:], c0_raw[:, :, hi])
+        quantize_into(c_q[0], hi, c0_g[1])
+        quantize_into(c_q[0], lo, c0_g[0])
+        for j in range(4):
+            mm(j, c_q[0], u_q[0][0][:].bitcast(FP8X4), u_q[0][1][:], False, False)
+
+        u1_g = [grouped_tile(f"u1_g{h}", HALF) for h in range(2)]
+        interleave("s", u1_g[0][:], u1_raw[:, :, lo])
+        interleave("v", u1_g[1][:], u1_raw[:, :, hi])
+        quantize_into(u_q[1], hi, u1_g[1])
+        quantize_into(u_q[1], lo, u1_g[0])
+
+        def last_pass(j):
+            mm(j, c_q[1], u_q[1][0][:].bitcast(FP8X4), u_q[1][1][:], False, True)
+
+        total = [keep.tile([P, M], F32, name=f"total{j}") for j in range(4)]
+        res = [keep.tile([P, M], F32, name=f"res{j}") for j in range(4)]
+
+        def finish(j, pieces):
+            w = M // pieces
+            for n in range(pieces):
+                cols = slice(w * n, w * (n + 1))
+                nc.vector.tensor_tensor(total[j][:, cols], acc[j][:, cols], bias[:, cols], ADD)
+                nc.scalar.activation(res[j][:, cols], total[j][:, cols], GELU)
+            nc.sync.dma_start(out=out[J * j : J * (j + 1), :], in_=res[j][:])
+
+        c1_g = [grouped_tile(f"c1_g{n}", J) for n in range(4)]
+        interleave("v", c1_g[0][:], c1_raw[0][:, :, 0:J])
+        interleave("s", c1_g[1][:], c1_raw[0][:, :, J : 2 * J])
+        quantize_into(c_q[1], slice(0, J), c1_g[0])
+        quantize_into(c_q[1], slice(J, 2 * J), c1_g[1])
+        last_pass(0)
+        last_pass(1)
+        interleave("v", c1_g[2][:], c1_raw[1][:])
+        quantize_into(c_q[1], slice(2 * J, 3 * J), c1_g[2])
+        last_pass(2)
+        interleave("v", c1_g[3][:], c1_raw[2][:])
+        quantize_into(c_q[1], slice(3 * J, 4 * J), c1_g[3])
+        last_pass(3)
+        finish(0, 1)
+        finish(1, 1)
+        finish(2, 1)
+        finish(3, 2)

@@ -46,6 +46,17 @@ def tile_list_hmix_tm_gelu_kernel(tc, xT, w4_words, w4_scales, c, u, wgt, b, off
                 out=codes.bitcast(FP8X4), scales=scales, in_=grouped.rearrange("p w i -> p (w i)")
             )
 
+        w4_sc = keep.tile([P, M], U8, name="w4_sc", align_bytes=64)
+        nc.gpsimd.memset(w4_sc[:].bitcast(I32), 0)
+        b_rows = keep.tile([P, P], F32, name="b_rows")
+        nc.gpsimd.memset(b_rows[:], 0.0)
+        for q in range(4):
+            nc.scalar.dma_start(
+                out=w4_sc[32 * q : 32 * q + 4, :].bitcast(I32),
+                in_=w4_scales[0, 4 * q : 4 * q + 4, :].bitcast(I32),
+            )
+        nc.scalar.dma_start(out=b_rows[0:4, :], in_=b.rearrange("(m n) -> m n", n=P))
+
         offsets = lists.tile([P, S // 16], U16, name="offsets")
         nc.sync.dma_start(offsets[:], offs)
         wgt_sb = keep.tile([P, S], F32, name="wgt_sb")
@@ -63,10 +74,6 @@ def tile_list_hmix_tm_gelu_kernel(tc, xT, w4_words, w4_scales, c, u, wgt, b, off
             nc.sync.dma_start(out=t[:], in_=rows)
             return t
 
-        w4_sc = keep.tile([P, M], U8, name="w4_sc", align_bytes=64)
-        nc.gpsimd.memset(w4_sc[:].bitcast(I32), 0)
-        b_rows = keep.tile([P, P], F32, name="b_rows")
-        nc.gpsimd.memset(b_rows[:], 0.0)
         ident = keep.tile([P, P], F32, name="ident")
         make_identity(nc, ident[:])
 
@@ -74,15 +81,9 @@ def tile_list_hmix_tm_gelu_kernel(tc, xT, w4_words, w4_scales, c, u, wgt, b, off
         u0_raw = load_rows("u0_raw", u, 0, slice(0, M))
         load_plane(1)
         load_plane(2)
+        load_plane(3)
         w4_sb = keep.tile([P, 2 * M], U8, name="w4_sb", align_bytes=64)
         nc.sync.dma_start(out=w4_sb[:].bitcast(I32), in_=w4_words[0].bitcast(I32))
-        for q in range(4):
-            nc.sync.dma_start(
-                out=w4_sc[32 * q : 32 * q + 4, :].bitcast(I32),
-                in_=w4_scales[0, 4 * q : 4 * q + 4, :].bitcast(I32),
-            )
-        nc.sync.dma_start(out=b_rows[0:4, :], in_=b.rearrange("(m n) -> m n", n=P))
-        load_plane(3)
         c0_raw = load_rows("c0_raw", c, 0, slice(0, S))
         u1_raw = load_rows("u1_raw", u, 1, slice(0, M))
         c1_cols = [slice(0, 256), slice(256, 384), slice(384, 512)]
@@ -109,6 +110,15 @@ def tile_list_hmix_tm_gelu_kernel(tc, xT, w4_words, w4_scales, c, u, wgt, b, off
         def quantize_into(q, cols, grouped):
             quantize(q[0][:, cols], q[1][:, cols], grouped[:])
 
+        def shared(name, q, first, raw, cut):
+            w = raw.shape[2]
+            g = grouped_tile(name, w)
+            if cut > 0:
+                interleave("s", g[:, 0:cut, :], raw[:, :, 0:cut])
+            if cut < w:
+                interleave("v", g[:, cut:w, :], raw[:, :, cut:w])
+            quantize_into(q, slice(first, first + w), g)
+
         picked = [keep.tile([P, PACK, HALF], F32, name=f"picked{h}") for h in range(2)]
 
         def gather(i, h):
@@ -123,11 +133,9 @@ def tile_list_hmix_tm_gelu_kernel(tc, xT, w4_words, w4_scales, c, u, wgt, b, off
 
         gather(0, 0)
         gather(0, 1)
-        u0_g = grouped_tile("u0_g", 512)
-        interleave("s", u0_g[:], u0_raw[:])
+        shared("u0_g", u_q[0], 0, u0_raw, 512)
         gather(1, 0)
         gather(1, 1)
-        quantize_into(u_q[0], slice(0, 512), u0_g)
         gather(2, 0)
         gather(2, 1)
 
@@ -168,19 +176,11 @@ def tile_list_hmix_tm_gelu_kernel(tc, xT, w4_words, w4_scales, c, u, wgt, b, off
         for j in range(4):
             mm(j, xg_q, w4_sb[:].bitcast(FP4X4), w4_sc[:], True, False)
 
-        c0_g = [grouped_tile(f"c0_g{h}", HALF) for h in range(2)]
-        interleave("s", c0_g[0][:], c0_raw[:, :, lo])
-        interleave("v", c0_g[1][:], c0_raw[:, :, hi])
-        quantize_into(c_q[0], hi, c0_g[1])
-        quantize_into(c_q[0], lo, c0_g[0])
+        shared("c0_g", c_q[0], 0, c0_raw, 256)
         for j in range(4):
             mm(j, c_q[0], u_q[0][0][:].bitcast(FP8X4), u_q[0][1][:], False, False)
 
-        u1_g = [grouped_tile(f"u1_g{h}", HALF) for h in range(2)]
-        interleave("s", u1_g[0][:], u1_raw[:, :, lo])
-        interleave("v", u1_g[1][:], u1_raw[:, :, hi])
-        quantize_into(u_q[1], hi, u1_g[1])
-        quantize_into(u_q[1], lo, u1_g[0])
+        shared("u1_g", u_q[1], 0, u1_raw, 192)
 
         def last_pass(j):
             mm(j, c_q[1], u_q[1][0][:].bitcast(FP8X4), u_q[1][1][:], False, True)
@@ -194,22 +194,13 @@ def tile_list_hmix_tm_gelu_kernel(tc, xT, w4_words, w4_scales, c, u, wgt, b, off
                 cols = slice(w * n, w * (n + 1))
                 nc.vector.tensor_tensor(total[j][:, cols], acc[j][:, cols], bias[:, cols], ADD)
                 nc.scalar.activation(res[j][:, cols], total[j][:, cols], GELU)
-            nc.sync.dma_start(out=out[J * j : J * (j + 1), :], in_=res[j][:])
+                nc.sync.dma_start(out=out[J * j : J * (j + 1), cols], in_=res[j][:, cols])
 
-        c1_g = [grouped_tile(f"c1_g{n}", J) for n in range(4)]
-        interleave("v", c1_g[0][:], c1_raw[0][:, :, 0:J])
-        interleave("s", c1_g[1][:], c1_raw[0][:, :, J : 2 * J])
-        quantize_into(c_q[1], slice(0, J), c1_g[0])
-        quantize_into(c_q[1], slice(J, 2 * J), c1_g[1])
-        last_pass(0)
-        last_pass(1)
-        interleave("v", c1_g[2][:], c1_raw[1][:])
-        quantize_into(c_q[1], slice(2 * J, 3 * J), c1_g[2])
-        last_pass(2)
-        interleave("v", c1_g[3][:], c1_raw[2][:])
-        quantize_into(c_q[1], slice(3 * J, 4 * J), c1_g[3])
-        last_pass(3)
-        finish(0, 1)
-        finish(1, 1)
-        finish(2, 1)
-        finish(3, 2)
+        c1_engines = ("v", "s", "s", "v")
+        for j, engine in enumerate(c1_engines):
+            n = (0, 0, 1, 2)[j]
+            at = J * j - c1_cols[n].start
+            shared(f"c1_g{j}", c_q[1], J * j, c1_raw[n][:, :, at : at + J], J if engine == "s" else 0)
+            last_pass(j)
+        for j, pieces in enumerate((1, 1, 1, 2)):
+            finish(j, pieces)

@@ -86,8 +86,7 @@ def tile_list_hmix_tm_gelu_kernel(tc, xT, w4_words, w4_scales, c, u, wgt, b, off
         nc.sync.dma_start(out=w4_sb[:].bitcast(I32), in_=w4_words[0].bitcast(I32))
         c0_raw = load_rows("c0_raw", c, 0, slice(0, S))
         u1_raw = load_rows("u1_raw", u, 1, slice(0, M))
-        c1_cols = [slice(0, 256), slice(256, 384), slice(384, 512)]
-        c1_raw = [load_rows(f"c1_raw{n}", c, 1, cols) for n, cols in enumerate(c1_cols)]
+        c1_raw = [load_rows(f"c1_raw{j}", c, 1, slice(J * j, J * (j + 1))) for j in range(4)]
 
         warm = keep.tile([P, 1], F32, name="warm")
         nc.vector.memset(warm[:], 0.0)
@@ -133,7 +132,7 @@ def tile_list_hmix_tm_gelu_kernel(tc, xT, w4_words, w4_scales, c, u, wgt, b, off
 
         gather(0, 0)
         gather(0, 1)
-        shared("u0_g", u_q[0], 0, u0_raw, 512)
+        shared("u0_g", u_q[0], 0, u0_raw, 256)
         gather(1, 0)
         gather(1, 1)
         gather(2, 0)
@@ -180,7 +179,7 @@ def tile_list_hmix_tm_gelu_kernel(tc, xT, w4_words, w4_scales, c, u, wgt, b, off
         for j in range(4):
             mm(j, c_q[0], u_q[0][0][:].bitcast(FP8X4), u_q[0][1][:], False, False)
 
-        shared("u1_g", u_q[1], 0, u1_raw, 192)
+        shared("u1_g", u_q[1], 0, u1_raw, 160)
 
         def last_pass(j):
             mm(j, c_q[1], u_q[1][0][:].bitcast(FP8X4), u_q[1][1][:], False, True)
@@ -196,11 +195,8 @@ def tile_list_hmix_tm_gelu_kernel(tc, xT, w4_words, w4_scales, c, u, wgt, b, off
                 nc.scalar.activation(res[j][:, cols], total[j][:, cols], GELU)
                 nc.sync.dma_start(out=out[J * j : J * (j + 1), cols], in_=res[j][:, cols])
 
-        c1_engines = ("v", "s", "s", "v")
-        for j, engine in enumerate(c1_engines):
-            n = (0, 0, 1, 2)[j]
-            at = J * j - c1_cols[n].start
-            shared(f"c1_g{j}", c_q[1], J * j, c1_raw[n][:, :, at : at + J], J if engine == "s" else 0)
+        for j, cut in enumerate((96, 32, 128, 32)):
+            shared(f"c1_g{j}", c_q[1], J * j, c1_raw[j], cut)
             last_pass(j)
-        for j, pieces in enumerate((1, 1, 1, 2)):
+        for j, pieces in enumerate((2, 2, 2, 2)):
             finish(j, pieces)

@@ -78,12 +78,12 @@ def tile_list_hmix_tm_gelu_kernel(tc, xT, w4_words, w4_scales, c, u, wgt, b, off
         make_identity(nc, ident[:])
 
         load_plane(0)
-        u0_raw = load_rows("u0_raw", u, 0, slice(0, M))
         load_plane(1)
         load_plane(2)
         load_plane(3)
         w4_sb = keep.tile([P, 2 * M], U8, name="w4_sb", align_bytes=64)
         nc.sync.dma_start(out=w4_sb[:].bitcast(I32), in_=w4_words[0].bitcast(I32))
+        u0_raw = load_rows("u0_raw", u, 0, slice(0, M))
         c0_raw = load_rows("c0_raw", c, 0, slice(0, S))
         u1_raw = load_rows("u1_raw", u, 1, slice(0, M))
         c1_raw = [load_rows(f"c1_raw{j}", c, 1, slice(J * j, J * (j + 1))) for j in range(4)]
@@ -132,7 +132,6 @@ def tile_list_hmix_tm_gelu_kernel(tc, xT, w4_words, w4_scales, c, u, wgt, b, off
 
         gather(0, 0)
         gather(0, 1)
-        shared("u0_g", u_q[0], 0, u0_raw, 256)
         gather(1, 0)
         gather(1, 1)
         gather(2, 0)
@@ -175,11 +174,12 @@ def tile_list_hmix_tm_gelu_kernel(tc, xT, w4_words, w4_scales, c, u, wgt, b, off
         for j in range(4):
             mm(j, xg_q, w4_sb[:].bitcast(FP4X4), w4_sc[:], True, False)
 
+        shared("u0_g", u_q[0], 0, u0_raw, 320)
         shared("c0_g", c_q[0], 0, c0_raw, 256)
         for j in range(4):
             mm(j, c_q[0], u_q[0][0][:].bitcast(FP8X4), u_q[0][1][:], False, False)
 
-        shared("u1_g", u_q[1], 0, u1_raw, 160)
+        shared("u1_g", u_q[1], 0, u1_raw, 192)
 
         def last_pass(j):
             mm(j, c_q[1], u_q[1][0][:].bitcast(FP8X4), u_q[1][1][:], False, True)

from contextlib import ExitStack

import concourse.mybir as mybir
from concourse.masks import make_identity

K, L, M, T, S = 512, 1024, 512, 2048, 512
FLOPS = 2 * S * M * (K + L)

F32 = mybir.dt.float32
BF16 = mybir.dt.bfloat16
I32 = mybir.dt.int32
U32 = mybir.dt.uint32
U16 = mybir.dt.uint16
U8 = mybir.dt.uint8
FP8X4 = mybir.dt.float8_e4m3fn_x4
FP4X4 = mybir.dt.float4_e2m1fn_x4
ADD = mybir.AluOpType.add
MULT = mybir.AluOpType.mult
COPY = mybir.ActivationFunctionType.Copy
GELU = mybir.ActivationFunctionType.Gelu_apprx_tanh

P = 128
PACK = 4
KP = P * PACK
HALF = 256
J = 128


def tile_list_hmix_tm_gelu_kernel(tc, xT, w4_words, w4_scales, c, u, wgt, b, offs, out):
    nc = tc.nc
    with ExitStack() as ctx:
        lists = ctx.enter_context(tc.tile_pool(name="lists", bufs=1))
        keep = ctx.enter_context(tc.tile_pool(name="keep", bufs=1))
        psum = ctx.enter_context(tc.psum_pool(name="psum", bufs=1))

        def interleave(engine, dst, src):
            o = dst.rearrange("p (a e) i -> p a i e", e=4)
            s = src.rearrange("p i (a e) -> p a i e", e=4)
            if engine == "v":
                nc.vector.tensor_copy(out=o, in_=s)
            else:
                nc.scalar.activation(o, s, COPY)

        def quantize(codes, scales, grouped):
            nc.vector.quantize_mx(
                out=codes.bitcast(FP8X4), scales=scales, in_=grouped.rearrange("p w i -> p (w i)")
            )

        w4_sc = keep.tile([P, M], U8, name="w4_sc", align_bytes=64)
        nc.gpsimd.memset(w4_sc[:].bitcast(I32), 0)
        b_rows = keep.tile([P, P], F32, name="b_rows")
        nc.gpsimd.memset(b_rows[:], 0.0)
        for q in range(4):
            nc.scalar.dma_start(
                out=w4_sc[32 * q : 32 * q + 4, :].bitcast(I32),
                in_=w4_scales[0, 4 * q : 4 * q + 4, :].bitcast(I32),
            )
        nc.scalar.dma_start(out=b_rows[0:4, :], in_=b.rearrange("(m n) -> m n", n=P))

        offsets = lists.tile([P, S // 16], U16, name="offsets")
        nc.sync.dma_start(offsets[:], offs)
        wgt_sb = keep.tile([P, S], F32, name="wgt_sb")
        nc.sync.dma_start(out=wgt_sb[:], in_=wgt)

        x_rows = xT.rearrange("(p i) t -> p i t", i=PACK)
        planes = [keep.tile([P, T], F32, name=f"plane{i}") for i in range(PACK)]

        def load_plane(i):
            nc.sync.dma_start(out=planes[i][:], in_=x_rows[:, i, :])

        def load_rows(name, src, a, cols):
            t = keep.tile([P, PACK, cols.stop - cols.start], F32, name=name)
            rows = src[a * KP : (a + 1) * KP, cols].rearrange("(p i) w -> p i w", i=PACK)
            nc.sync.dma_start(out=t[:], in_=rows)
            return t

        ident = keep.tile([P, P], F32, name="ident")
        make_identity(nc, ident[:])

        load_plane(0)
        load_plane(1)
        load_plane(2)
        load_plane(3)
        w4_sb = keep.tile([P, 2 * M], U8, name="w4_sb", align_bytes=64)
        nc.sync.dma_start(out=w4_sb[:].bitcast(I32), in_=w4_words[0].bitcast(I32))
        u0_raw = load_rows("u0_raw", u, 0, slice(0, M))
        c0_raw = load_rows("c0_raw", c, 0, slice(0, S))
        u1_raw = load_rows("u1_raw", u, 1, slice(0, M))
        c1_raw = [load_rows(f"c1_raw{j}", c, 1, slice(J * j, J * (j + 1))) for j in range(4)]

        warm = keep.tile([P, 1], F32, name="warm")
        nc.vector.memset(warm[:], 0.0)
        warm_out = keep.tile([P, 1], F32, name="warm_out")
        nc.scalar.activation(warm_out[:], warm[:], GELU)

        def codes_and_scales(name):
            return (
                keep.tile([P, 512], U32, name=name + "_codes", align_bytes=64),
                keep.tile([P, 512], U8, name=name + "_scales", align_bytes=64),
            )

        xg_q = codes_and_scales("xg")
        u_q = [codes_and_scales(f"u{a}") for a in range(2)]
        c_q = [codes_and_scales(f"c{a}") for a in range(2)]

        def grouped_tile(name, w):
            return keep.tile([P, w, PACK], BF16, name=name, align_bytes=64)

        def quantize_into(q, cols, grouped):
            quantize(q[0][:, cols], q[1][:, cols], grouped[:])

        def shared(name, q, first, raw, cut):
            w = raw.shape[2]
            g = grouped_tile(name, w)
            if cut > 0:
                interleave("s", g[:, 0:cut, :], raw[:, :, 0:cut])
            if cut < w:
                interleave("v", g[:, cut:w, :], raw[:, :, cut:w])
            quantize_into(q, slice(first, first + w), g)

        picked = [keep.tile([P, PACK, HALF], F32, name=f"picked{h}") for h in range(2)]

        def gather(i, h):
            nc.vector.tensor_tensor(
                picked[h][:, i, :],
                planes[i][:].indirect(offsets[:, 16 * h : 16 * (h + 1)]),
                wgt_sb[:, HALF * h : HALF * (h + 1)],
                MULT,
            )

        lo, hi = slice(0, HALF), slice(HALF, 512)

        gather(0, 0)
        gather(0, 1)
        gather(1, 0)
        gather(1, 1)
        gather(2, 0)
        gather(2, 1)

        b_bank = psum.tile([P, 512], F32, name="b_bank")
        nc.tensor.transpose(b_bank[:, 0:P], b_rows[:], ident[:])
        b_col = keep.tile([P, 4], F32, name="b_col")
        nc.scalar.copy(b_col[:], b_bank[:, 0:4])
        b_bank2 = psum.tile([P, 512], F32, name="b_bank2")
        for m in range(4):
            nc.tensor.transpose(
                b_bank2[:, P * m : P * (m + 1)], b_col[:, m : m + 1].to_broadcast([P, P]), ident[:]
            )
        bias = keep.tile([P, M], F32, name="bias")
        nc.scalar.copy(bias[:], b_bank2[:])

        gather(3, 0)
        xg_g = [grouped_tile(f"xg_g{h}", HALF) for h in range(2)]
        interleave("s", xg_g[0][:], picked[0][:])
        gather(3, 1)
        interleave("v", xg_g[1][:], picked[1][:])
        quantize_into(xg_q, lo, xg_g[0])
        quantize_into(xg_q, hi, xg_g[1])

        acc = [psum.tile([P, M], F32, name=f"acc{j}") for j in range(4)]

        def mm(j, stat, mov, mov_scale, start, stop):
            js = slice(J * j, J * (j + 1))
            nc.tensor.matmul_mx(
                out=acc[j][:],
                lhsT=stat[0][:, js].bitcast(FP8X4),
                lhsT_scale=stat[1][:, js],
                rhs=mov,
                rhs_scale=mov_scale,
                start=start,
                stop=stop,
            )

        for j in range(4):
            mm(j, xg_q, w4_sb[:].bitcast(FP4X4), w4_sc[:], True, False)

        shared("u0_g", u_q[0], 0, u0_raw, 320)
        shared("c0_g", c_q[0], 0, c0_raw, 256)
        for j in range(4):
            mm(j, c_q[0], u_q[0][0][:].bitcast(FP8X4), u_q[0][1][:], False, False)

        shared("u1_g", u_q[1], 0, u1_raw, 192)

        def last_pass(j):
            mm(j, c_q[1], u_q[1][0][:].bitcast(FP8X4), u_q[1][1][:], False, True)

        total = [keep.tile([P, M], F32, name=f"total{j}") for j in range(4)]
        res = [keep.tile([P, M], F32, name=f"res{j}") for j in range(4)]

        def finish(j, pieces):
            w = M // pieces
            for n in range(pieces):
                cols = slice(w * n, w * (n + 1))
                nc.vector.tensor_tensor(total[j][:, cols], acc[j][:, cols], bias[:, cols], ADD)
                nc.scalar.activation(res[j][:, cols], total[j][:, cols], GELU)
                nc.sync.dma_start(out=out[J * j : J * (j + 1), cols], in_=res[j][:, cols])

        for j, cut in enumerate((96, 32, 128, 32)):
            shared(f"c1_g{j}", c_q[1], J * j, c1_raw[j], cut)
            last_pass(j)
        for j, pieces in enumerate((2, 2, 2, 2)):
            finish(j, pieces)
